import numpy as np, ml_dtypes
CORES = [5,29,101,125,133,157,229,253]
N = 8
import mx_ref
BF = ml_dtypes.bfloat16
def entries(a):
    return np.ascontiguousarray(a.T).reshape(-1)
def table(e):
    return np.ascontiguousarray(np.reshape(e, (-1, 16)).T).astype(np.int32)
def cols(t, e):
    v = np.concatenate([t.reshape(128, -1, 4), np.zeros((128, 1, 4), BF)], axis=1)
    return np.ascontiguousarray(v[:, e]).reshape(128, -1)
def f(rng, *shape):
    return mx_ref.flush((rng.standard_normal(shape, dtype=np.float32) * np.exp2(rng.integers(-2, 3, shape[:-1] + (1,)))).astype(BF))
def wide(rng, *shape, cols=0):
    v = rng.standard_normal(shape, dtype=np.float32) * np.exp2(rng.integers(-12, 13, shape)).astype(np.float32)
    if cols: v *= np.repeat(np.exp2(rng.integers(-cols, cols + 1, shape[:-2] + (1, shape[-1] // 4))) * (rng.random(shape[:-2] + (1, shape[-1] // 4)) > 0.0625), 4, axis=-1).astype(np.float32)
    return mx_ref.flush(v.astype(BF))
T, O = 128, 4
CAP, ROOM = 144, 160
PAIR, MOVE, BOTH = 24, 8, 30
def turn(v, e):
    v = np.sort(v); return v[np.argsort((v // T - e) % N, kind="stable")]
def play(c1, c2):
    a, b = c1.reshape(-1), c2.reshape(-1)
    first = [turn(np.flatnonzero(a == e), e)[:CAP] for e in range(N)]
    refused = np.setdiff1d(np.arange(N * T), np.concatenate(first))
    second = [turn(refused[b[refused] == e], e)[:ROOM - len(first[e])] for e in range(N)]
    return first, second, refused
def broken(c1, c2):
    b = []
    if c1.min() < 0 or c1.max() >= N: return ["c1"]
    if c2.min() < 0 or c2.max() >= N: return ["c2"]
    if (c1 == c2).any(): b.append("a token with two equal choices")
    if max(np.bincount(v, minlength=N).max() for v in c1) > PAIR: b.append("first choices of a pair of ranks")
    first, second, refused = play(c1, c2)
    if np.bincount(c1.reshape(-1)[refused] * N + c2.reshape(-1)[refused], minlength=N * N).max() > MOVE: b.append("refused tokens of a pair of ranks")
    for e in range(N):
        if np.bincount(np.concatenate([first[e], second[e]]) // T, minlength=N).max() > BOTH: b.append("admitted tokens of a pair of ranks")
    return b
def fill(rng, low, high, total):
    n, p = np.array(low), rng.dirichlet(np.full(len(low), 16.0))
    while n.sum() < total: n = np.minimum(n + rng.multinomial(total - n.sum(), p), high)
    return n
def deal(rng, tot):
    n = np.stack([np.bincount(v, minlength=N) for v in rng.permutation(np.repeat(np.arange(N), tot)).reshape(N, T)])
    while n.max() > PAIR:
        s, e = np.argwhere(n > PAIR)[0]
        q = rng.choice(np.flatnonzero(n[:, e] < PAIR))
        g = rng.choice(np.flatnonzero(n[q] > n[s]))
        n[s, e] -= 1; n[q, e] += 1; n[q, g] -= 1; n[s, g] += 1
    return n
def bounds():
    return np.full(N, T >> 3), np.full(N, N * PAIR), np.zeros((N, N), int), MOVE * (1 - np.eye(N, dtype=int))
def lists(rng, low, high, mlow, mhigh, pair=None, skew=False, force=None):
    for _ in range(50):
        n = deal(rng, fill(rng, low, high, N * T))
        if pair or force:
            s, g, e = pair or (*force, force[1])
            for to in (g, e):
                while n[s, to] < PAIR:
                    h, q = [(h, q) for h in range(N) for q in range(N) if h not in (g, e) and n[s, h] > 0 and q != s and n[q, to] > 0 and n[q, h] < PAIR][0]
                    n[s, to] += 1; n[s, h] -= 1; n[q, to] -= 1; n[q, h] += 1
        c1 = np.concatenate([rng.permutation(np.repeat(np.arange(N), v)) for v in n])
        c2 = (c1 + rng.integers(1, N, N * T)) % N
        for e in range(N):
            at = turn(np.flatnonzero(c1 == e), e)[CAP:]
            c2[at] = rng.permutation(np.repeat(np.arange(N), fill(rng, mlow[e], mhigh[e], len(at))))
            if pair and e == pair[1]:
                mine = at[at // T == pair[0]]; named = c2[at]
                named = np.concatenate([named[named == pair[2]], named[named != pair[2]]]); k = int((named == pair[2]).sum())
                to = rng.permutation(mine)[:k]; c2[np.setdiff1d(at, to)] = named[k:]; c2[to] = pair[2]
        if skew:
            out = np.zeros(N * T, bool)
            for e in range(N): out[turn(np.flatnonzero(c1 == e), e)[CAP:]] = True
            for s in range(N):
                e = (s + rng.integers(3, N)) % N; k = np.arange(s * T, s * T + T)
                k = k[~out[k] & ((c1[k] - s - 1) % N < 2)]; c2[k] = e
        c1, c2 = c1.reshape(N, T), c2.reshape(N, T)
        if not broken(c1, c2): return {"c1": np.stack([table(v) for v in c1]), "c2": np.stack([table(v) for v in c2])}
    raise RuntimeError("no lists found")
def tiles(rng):
    return {"x": f(rng, N, 128, 4 * T), "w": f(rng, N, 128, 512 * O)}
def setup_inputs(rng):
    return {**tiles(rng), **lists(rng, *bounds())}
def setup_inputs_pair(rng):
    low, high, mlow, mhigh = bounds()
    p = rng.permutation(N); g, e, z = p[0], p[1], p[2]; s = (g - 1) % N
    if s in (e, z): e, z = [k for k in p if k not in (g, s)][:2]
    few = N - 2 - (N > 4)
    high[:] = CAP + (few - 1 + (N == 4)) * MOVE
    low[g] = high[g] = CAP + min(PAIR, BOTH - PAIR + few * MOVE); low[e] = N * PAIR >> 2; high[e] = CAP
    mhigh[:, e] = 0; mlow[g, e] = mhigh[g, e] = BOTH - PAIR
    if N > 4: low[z] = high[z] = 0; mhigh[:, z] = 0
    return {**tiles(rng), **lists(rng, low, high, mlow, mhigh, (int(s), int(g), int(e)))}
def setup_inputs_exact(rng):
    low, high, mlow, mhigh = bounds()
    p = rng.permutation(N); src = p[2:2 + (ROOM - CAP) // MOVE]
    high[:] = CAP
    low[p[0]] = CAP
    low[p[1]] = high[p[1]] = CAP + 1
    low[p[-1]] = N * PAIR >> 2
    mhigh[:, p[-1]] = np.minimum(mhigh[:, p[-1]], MOVE >> 1)
    low[src] = high[src] = N * PAIR
    mhigh[:, p[0]] = 0
    mlow[src, p[0]] = mhigh[src, p[0]] = MOVE
    return {**tiles(rng), **lists(rng, low, high, mlow, mhigh, skew=True, force=(int(p[-1] - 1) % N, int(p[-1])))}
def setup_inputs_full(rng):
    low, high, mlow, mhigh = bounds()
    p = rng.permutation(N); src = p[1:1 + 2 * ((ROOM - CAP) // MOVE)]
    low[p[0]] = CAP + 3 * MOVE // 2
    low[src] = CAP + MOVE
    mlow[src, p[0]] = MOVE
    return {**tiles(rng), **lists(rng, low, high, mlow, mhigh)}
def setup_inputs_room(rng):
    low, high, mlow, mhigh = bounds()
    p = rng.permutation(N); src = p[1:2 + (ROOM - CAP) // MOVE]
    low[p[0]] = high[p[0]] = CAP - 1
    low[src] = CAP + MOVE
    mlow[src, p[0]] = MOVE
    return {**tiles(rng), **lists(rng, low, high, mlow, mhigh)}
def setup_inputs_spread(rng):
    d = setup_inputs(rng); d["x"] = wide(rng, N, 128, 4 * T, cols=6); return d
def check_inputs(d):
    return broken(np.stack([entries(v) for v in d["c1"]]), np.stack([entries(v) for v in d["c2"]]))
def reference(x, w, c1, c2):
    first, second, _ = play(np.stack([entries(v) for v in c1]), np.stack([entries(v) for v in c2]))
    tokens = np.concatenate([x[r] for r in range(N)], axis=1)
    y = np.zeros((N, 128, O * ROOM), np.float32)
    for e in range(N):
        held = np.concatenate([first[e], second[e]])
        t = mx_ref.quantize(cols(tokens, np.concatenate([held, np.full(ROOM - len(held), -1)])))
        for o in range(O): y[e][:, ROOM * o:ROOM * o + ROOM] = mx_ref.matmul(mx_ref.quantize(w[e][:, 512 * o:512 * o + 512]), t)
    return {"y": y}

@@ -1,0 +1,475 @@
+import numpy as np
+from concourse.bass import DstId, RemoteDMATransfer
+from concourse.mybir import dt, AluOpType, AxisListType, ActivationFunctionType
+
+N = 8
+CAP, ROOM, O = 144, 160, 4
+W = 32
+LAND = N * W
+
+F4, B2, I4, U2, MX, U1 = "float32", "bfloat16", "int32", "uint16", "float8_e4m3fn_x4", "uint8"
+SIZES = {
+    I4: dict(c1b=8, c2b=8, cm=8, cs=8, pi=1, kk=8, r1i=64, r2i=64, r1=64, r2=64),
+    U2: dict(cu=8, so=4, offp=16, offh=10),
+    F4: dict(kf=8, bo=32, bt=32, ic=32, k32=320, kp=320, x16=384, kr=384, jd=320, jw0=10, jw=10, val0=64, val=64,
+             sc0=16, sc1=16, scl=16, fc=48, cr=96, c2c=64, cda=32, cdb=32, ca=128, cb=128, ya1=128, yb1=128, ya=128, yb=128,
+             e1=96, e1t=96, e2=64, e2t=64, e2s=8, cum=128, mm=128, mt=128, ss=128, win=384, rr=384, vv=32, vt=32, v2=32,
+             vb=32, st=320, stt=320, sw=320, wl=10, ys=640),
+    B2: dict(tn=64, ta=64, tb=64, te=64, tia=64, tib=64, eq2=64, eqa=64, eqb=64, gn=128, ga=128, gb=128, ge=128, gia=128,
+             gib=128, xa=128, xb=128, xs=128,
+             info1=16, info2=16, hand1=4, hand2=4, land1=22, land2=22,
+             xt=512, wt=2048, zt=640),
+    MX: dict(xq=128, wq=512, oq=256, rq=64, lq=416, hq=160),
+    U1: dict(xz=128, wz=512, oz=256, rz=64, lz=416, hz=160),
+}
+SCRATCH = {"ps": ("psum", [128, 2048], F4)}
+for _d in SIZES:
+    for _n in SIZES[_d]:
+        SCRATCH[_n] = ("sbuf", [128, SIZES[_d][_n]], _d)
+SEMAPHORES = ["v", "a", "p", "ld", "lx", "lw", "ly", "i1", "i2", "tc", "ts", "lo", "pc1", "pc2", "pa1", "pa2", "n2",
+              "t0", "t1", "t2", "t3", "y0", "y1", "y2", "y3"]
+
+
+def bits(es):
+    m = 0
+    for e in es:
+        m |= 1 << e
+    return m
+
+
+def at(T, topo, s, u):
+    return T.cores[(s + u) % N]
+
+
+def order(T, topo, s):
+    cross = [u for u in range(1, N) if not topo.may_write(T.cores[s], at(T, topo, s, u))]
+    direct = [u for u in range(1, N) if u not in cross]
+    return cross, direct
+
+
+def relays(T, topo, s):
+    me = T.cores[s]
+    cross, _ = order(T, topo, s)
+    r = [c for c in topo.cores_of(me) if c != me and T.rank_of(c) is None
+         and all(topo.may_write(c, at(T, topo, s, u)) for u in cross)]
+    near = [c for c in r if topo.die(c) == topo.die(me)]
+    far = [c for c in r if topo.die(c) != topo.die(me)]
+    return [near[0], far[0]], [far[1], near[1]]
+
+
+SPLIT_C = ((0, 2), (2, 4), (4, 8))
+SPLIT_S = ((4, 6), (6, 8), (0, 4))
+
+
+def xfer(core, d, topo, es, sem, src, dst):
+    rid, pid = topo.addr(d, core)
+    return RemoteDMATransfer(dst_ids=[DstId(rid=rid, pnc=pid)], dma_engine_mask=bits(es), remote_sem=sem, src=src, dst=dst)
+
+
+def slot_of(u):
+    return (N - u) % N
+
+
+def hand_on(g, core, T, topo):
+    for s in range(N):
+        cross, _ = order(T, topo, s)
+        rc, rs = relays(T, topo, s)
+        for h in range(2):
+            us = cross[2 * h:2 * h + 2]
+            for kind, who in (("c", rc), ("s", rs)):
+                if who[h] != core:
+                    continue
+                es = [topo.engines(core, at(T, topo, s, u)) for u in us]
+                es = [es[0][0:4], es[1][4:8]]
+                isem, tsem = (T.sem.i1, T.sem.tc) if kind == "c" else (T.sem.i2, T.sem.ts)
+                hand, land = (T.hand1, T.land1) if kind == "c" else (T.hand2, T.land2)
+                g.wait_ge(isem, 4)
+                tr = []
+                for i, u in enumerate(us):
+                    c = 8 + 2 * (slot_of(u) - 1)
+                    tr.append(xfer(core, at(T, topo, s, u), topo, es[i], isem, hand[:, 2 * i:2 * i + 2], land[:, c:c + 2]))
+                g.remote_dma_fused(tr, local_sem=T.sem.lo)
+                g.wait_ge(tsem, 4)
+                tr = []
+                for i, u in enumerate(us):
+                    c = W * slot_of(u)
+                    if kind == "c":
+                        a, b = T.rq[:, W * i:W * i + W].bitcast(dt.uint8), T.lq[:, c:c + W].bitcast(dt.uint8)
+                    else:
+                        a, b = T.rz[:, W * i:W * i + W], T.lz[:, c:c + W]
+                    tr.append(xfer(core, at(T, topo, s, u), topo, es[i], tsem, a, b))
+                g.remote_dma_fused(tr, local_sem=T.sem.lo)
+                g.wait_ge(T.sem.lo, 16)
+                return
+
+
+def rank_program(g, core, T, topo):
+    s = T.rank_of(core)
+    if s is None:
+        hand_on(g, core, T, topo)
+        return
+    A, X = AluOpType, AxisListType.X
+    Copy = ActivationFunctionType.Copy
+    sem = T.sem
+    vec, act, ten = g.vector, g.scalar, g.tensor
+    cross, direct = order(T, topo, s)
+    ords = [0] + cross + direct
+    rc, rs = relays(T, topo, s)
+
+    vn, vw = [0], [0]
+
+    def V(ins):
+        ins.then_inc(sem.v, 1)
+        vn[0] += 1
+
+    def fence():
+        if vw[0] < vn[0]:
+            vec.wait_ge(sem.v, vn[0])
+            vw[0] = vn[0]
+        return vn[0]
+
+    def ts(out, in0, a, b, op0, op1=None):
+        if op1 is None:
+            V(vec.tensor_scalar(out, in0, a, None, op0))
+        else:
+            V(vec.tensor_scalar(out, in0, a, b, op0, op1))
+
+    def tt(out, a, b, op):
+        V(vec.tensor_tensor(out, a, b, op))
+
+    def cp(out, a):
+        V(vec.tensor_copy(out, a))
+
+    def fill(out, c):
+        V(vec.memset(out, c))
+
+    def scan(out, a, b, ini, op0):
+        V(vec.tensor_tensor_scan(out, a, b, ini, op0, A.add))
+
+    an = [0]
+
+    def S(ins):
+        ins.then_inc(sem.a, 1)
+        an[0] += 1
+
+    pn = [0]
+
+    def I(out, pattern, base, cm=0, f=True):
+        if f:
+            g.iota(out, pattern, base, cm, allow_small_or_imprecise_dtypes=True).then_inc(sem.p, 1)
+        else:
+            g.iota(out, pattern, base, cm).then_inc(sem.p, 1)
+        pn[0] += 1
+
+    for q in range(8):
+        g.sync.dma_start(T.c1b[16 * q:16 * q + 16, :], T.c1[:, :]).then_inc(sem.ld, 16)
+        act.dma_start(T.c2b[16 * q:16 * q + 16, :], T.c2[:, :]).then_inc(sem.ld, 16)
+    g.sync.dma_start(T.xt[:, :], T.x[:, :]).then_inc(sem.lx, 16)
+
+    I(T.pi[:, :], [[0, 1]], 0, 1, False)
+    k = 0
+    while k < N:
+        n = 1
+        step = ords[k + 1] - ords[k] if k + 1 < N else 0
+        while k + n < N and ords[k + n] - ords[k + n - 1] == step:
+            n += 1
+        I(T.bo[:, k:k + n], [[step, n]], ords[k])
+        k += n
+    I(T.r1i[:, :], [[1, 8], [0, 8]], 8 - s, 0, False)
+    I(T.r2i[:, :], [[0, 8], [1, 8]], 8 - s, 0, False)
+    p1 = pn[0]
+
+    fc = lambda i: T.fc[:, i:i + 1]
+    KAP8, TY, K32, R16, HALF = [T.kf[:, i:i + 1] for i in range(5)]
+    UO = T.bt[:, 0:1]
+    k1, k2 = ords.index(1), ords.index(2)
+
+    fill(T.cr[:, :], 0.0)
+    fence()
+    fill(T.cr[:, k1:k1 + 1], 1.0)
+    fill(T.cr[:, 8:16], -1.0)
+    fill(T.cr[:, 32 + k2:33 + k2], 1.0)
+    fill(T.cr[:, 72:80], -1.0)
+    vec.wait_ge(sem.p, p1)
+    ts(T.kk[:, 0:1], T.pi[:, :], 7, None, A.bitwise_and)
+    ts(T.kk[:, 1:2], T.pi[:, :], 3, 3, A.logical_shift_right, A.bitwise_and)
+    ts(T.kk[:, 2:3], T.pi[:, :], 31, None, A.bitwise_and)
+    ts(T.kk[:, 3:4], T.pi[:, :], 15, None, A.bitwise_and)
+    ts(T.kk[:, 4:5], T.pi[:, :], 4, 1, A.logical_shift_right, A.bitwise_and)
+    ts(T.r1[:, :], T.r1i[:, :], 7, None, A.bitwise_and)
+    ts(T.r2[:, :], T.r2i[:, :], 7, None, A.bitwise_and)
+    cp(T.bo[:, 8:16], T.bo[:, 0:8])
+    fence()
+    cp(T.kf[:, 0:5], T.kk[:, 0:5])
+    cp(T.bo[:, 16:32], T.bo[:, 0:16])
+    fence()
+    V(vec.transpose(T.bt[:, :], T.bo[:, :]))
+    fence()
+    ts(fc(0), TY, 1.0, UO, A.add, A.add)
+    fence()
+    ts(fc(1), fc(0), 8.0, -8.0, A.is_equal, A.mult)
+    fence()
+    tt(fc(2), fc(0), fc(1), A.add)
+    fence()
+    ts(T.tn[:, :], T.r1[:, :], fc(2), None, A.is_equal)
+
+    vec.wait_ge(sem.ld, 256)
+    ts(T.cm[:, :], T.c1b[:, :], 8, None, A.mult)
+    fence()
+    tt(T.cs[:, :], T.cm[:, :], T.c2b[:, :], A.add)
+    fence()
+    cp(T.cu[:, :], T.cs[:, :])
+    fence()
+    cp(T.gn[:, :], T.tn[:, 0:64].indirect(T.cu[:, 0:8]))
+    fence()
+    V(vec.tensor_reduce(fc(3), T.gn[:, :], X, A.add))
+    fence()
+    ts(T.e1[:, :], T.cr[:, :], fc(3), None, A.mult)
+    fence()
+    V(vec.transpose(T.e1t[:, :], T.e1[:, :]))
+    fence()
+    tt(T.info1[:, 0:16:2], T.e1t[:, 0:8], T.e1t[:, 40:48], A.add)
+    cp(T.info1[:, 1:16:2], T.e1t[:, 72:80])
+    m1 = fence()
+
+    off = topo.engines(core, at(T, topo, s, direct[0]))
+    on = [e for e in topo.engines(core, rc[0]) if e not in off]
+    half = [on[0:4], on[4:8]]
+
+    def send_info(info, hand, land, isem, who):
+        tr = [xfer(core, who[h], topo, half[h], isem, info[:, 2 + 4 * h:6 + 4 * h], hand[:, :]) for h in range(2)]
+        g.remote_dma_fused(tr, local_sem=sem.lo)
+        tr = []
+        for i, u in enumerate(direct):
+            b = 2 * ords.index(u)
+            c = 8 + 2 * (slot_of(u) - 1)
+            tr.append(xfer(core, at(T, topo, s, u), topo, off[2 * i:2 * i + 2], isem, info[:, b:b + 2], land[:, c:c + 2]))
+        g.remote_dma_fused(tr, local_sem=sem.lo)
+
+    I(T.ic[:, :], [[1, 32]], 0)
+    I(T.x16[:, :], [[0, 24], [1, 16]], 0)
+    g.wait_ge(sem.v, m1)
+    send_info(T.info1, T.hand1, T.land1, sem.i1, rc)
+    I(T.k32[:, :], [[0, 10], [1, 32]], 0)
+    I(T.val0[:, :], [[32, 4], [1, 16]], 0)
+    I(T.jw0[:, :], [[16, 10]], 0)
+    I(T.jd[:, :], [[16, 10], [0, 2], [1, 16]], 0)
+    p2 = pn[0]
+
+    ISS, ISF, ISN = fc(4), fc(5), fc(6)
+    ts(ISS, TY, 1.0, None, A.is_equal)
+    ts(ISF, TY, 0.0, None, A.is_equal)
+    ts(ISN, TY, 2.0, None, A.is_equal)
+    ts(fc(7), UO, -1.0, 1.0, A.mult, A.add)
+    ts(T.te[:, :], T.r1[:, :], UO, None, A.is_equal)
+    ts(T.tb[:, :], T.r1[:, :], 2.0, None, A.is_equal)
+    ts(T.eq2[:, :], T.r2[:, :], UO, None, A.is_equal)
+    fence()
+    ts(fc(8), fc(7), ISS, UO, A.mult, A.add)
+    ts(fc(9), ISS, -1.0, 1.0, A.mult, A.add)
+    ts(T.eqb[:, :], T.eq2[:, :], ISS, None, A.mult)
+    fence()
+    ts(T.ta[:, :], T.r1[:, :], fc(8), None, A.is_equal)
+    ts(T.eqa[:, :], T.eq2[:, :], fc(9), None, A.max)
+    tt(T.tib[:, :], T.tb[:, :], T.eqb[:, :], A.mult)
+    fence()
+    tt(T.tia[:, :], T.ta[:, :], T.eqa[:, :], A.mult)
+    m2 = fence()
+
+    act.wait_ge(sem.v, m2)
+    for out, tab in ((T.ga, T.ta), (T.gb, T.tb), (T.gia, T.tia), (T.gib, T.tib), (T.ge, T.te)):
+        S(act.activation(out[:, :], tab[:, 0:64].indirect(T.cu[:, 0:8]), Copy))
+    a1 = an[0]
+    act.dma_start(T.wt[:, :], T.w[:, :]).then_inc(sem.lw, 16)
+
+    fill(T.zt[:, :], 0.0)
+    fill(T.land1[:, 0:8], 0.0)
+    fill(T.land2[:, 0:8], 0.0)
+    fill(T.win[:, :], 0.0)
+    fill(T.vv[:, :], 0.0)
+    tt(fc(10), ISS, ISF, A.subtract)
+    ts(fc(11), TY, -64.0, 174.0, A.mult, A.add)
+    ts(fc(12), KAP8, 48.0, -1.0, A.mult, A.add)
+    ts(fc(13), UO, -1.0, 8.0, A.mult, A.add)
+    ts(fc(14), UO, 0.0, -8.0, A.is_equal, A.mult)
+    ts(fc(15), HALF, 16.0, None, A.mult)
+    fence()
+    ts(T.land1[:, 0:1], ISS, 225.0, 30.0, A.mult, A.add)
+    fill(T.land1[:, 1:2], 255.0)
+    tt(fc(16), fc(13), fc(14), A.add)
+    fence()
+    ts(fc(17), TY, 8.0, fc(16), A.mult, A.add)
+    ts(fc(18), fc(16), -8.0, ISN, A.add, A.mult)
+    ts(fc(19), ISN, -8.0, 1.0, A.mult, A.add)
+    fence()
+    ts(fc(20), fc(18), 16.0, None, A.add)
+    tt(fc(21), fc(17), fc(19), A.add)
+    vec.wait_ge(sem.a, a1)
+    scan(T.ca[:, :], T.ga[:, :], T.zt[:, 0:128], 0.0, A.add)
+    scan(T.cb[:, :], T.gb[:, :], T.zt[:, 0:128], 0.0, A.add)
+    V(vec.tensor_reduce(fc(22), T.ge[:, :], X, A.add))
+    fence()
+    ts(T.ya1[:, :], T.ca[:, :], fc(10), fc(11), A.mult, A.add)
+    ts(T.yb1[:, :], T.cb[:, :], 110.0, None, A.add)
+    ts(fc(23), fc(22), ISS, fc(12), A.mult, A.add)
+    fence()
+    tt(T.ya[:, :], T.ya1[:, :], T.gia[:, :], A.mult)
+    tt(T.yb[:, :], T.yb1[:, :], T.gib[:, :], A.mult)
+    BASE = fc(23)
+    vec.wait_ge(sem.p, p2)
+    ts(T.c2c[:, 0:32], T.ic[:, :], fc(17), None, A.is_gt)
+    ts(T.cda[:, :], T.ic[:, :], fc(20), None, A.is_equal)
+    ts(T.cdb[:, :], T.ic[:, :], fc(21), None, A.is_equal)
+    ts(T.kp[:, :], T.k32[:, :], 1.0, None, A.min)
+    ts(T.kr[:, :], T.x16[:, :], R16, 256.0, A.is_gt, A.mult)
+    ts(T.sc0[:, :], T.x16[:, 0:16], R16, 1.0 / 256.0, A.is_gt, A.mult)
+    ts(T.sc1[:, :], T.x16[:, 0:16], R16, None, A.is_equal)
+    ts(T.val[:, :], T.val0[:, :], fc(15), None, A.add)
+    fence()
+    tt(T.c2c[:, 32:64], T.cda[:, :], T.cdb[:, :], A.subtract)
+    scan(T.scl[:, :], T.sc0[:, :], T.sc1[:, :], 0.0, A.mult)
+    vec.wait_ge(sem.lx, 16)
+    V(vec.quantize_mx(T.xq[:, 0:128], T.xz[:, 0:128], T.xt[:, :]))
+    fence()
+
+    n1 = 0
+    for u in range(1, N):
+        n1 += 2 if u in order(T, topo, (s - u) % N)[1] else 4
+    vec.wait_ge(sem.i1, n1)
+    V(vec.tensor_reduce(fc(24), T.land1[:, 0:22:2], X, A.add))
+    V(vec.tensor_reduce(fc(25), T.land1[:, 1:22:2], X, A.add))
+    fence()
+    ts(T.xa[:, :], T.ya[:, :], fc(24), None, A.is_ge)
+    ts(T.xb[:, :], T.yb[:, :], fc(25), None, A.is_ge)
+    fence()
+    scan(T.cum[:, :], T.xa[:, :], T.xb[:, :], BASE, A.add)
+    tt(T.xs[:, :], T.xa[:, :], T.xb[:, :], A.add)
+    fence()
+    ts(fc(26), T.cum[:, 127:128], BASE, None, A.subtract)
+    tt(T.mm[:, :], T.xs[:, :], T.cum[:, :], A.mult)
+    fence()
+    ts(T.e2[:, :], T.c2c[:, :], fc(26), None, A.mult)
+    V(vec.transpose(T.mt[:, :], T.mm[:, :]))
+    fence()
+    V(vec.transpose(T.e2t[:, :], T.e2[:, :]))
+    scan(T.ss[:, :], T.kp[:, 0:128], T.mt[:, :], 0.0, A.mult)
+    fence()
+    tt(T.info2[:, 0:16:2], T.e2t[:, 0:8], T.e2t[:, 8:16], A.add)
+    tt(T.e2s[:, :], T.e2t[:, 32:40], T.e2t[:, 40:48], A.add)
+    cp(T.so[:, :], T.ss[:, 15:128:32])
+    m3 = fence()
+    vec.tensor_tensor(T.info2[:, 1:16:2], T.e2s[:, :], T.e2t[:, 48:56], A.add).then_inc(sem.n2, 1)
+    cp(T.win[:, 0:384].indirect(T.so[:, 0:4]), T.val[:, :])
+    fence()
+    scan(T.rr[:, :], T.kr[:, :], T.win[:, :], 0.0, A.mult)
+    fence()
+    ts(T.vv[:, 0:16:2], T.rr[:, 15:384:48], T.scl[:, 15:16], None, A.mult)
+    ts(T.vv[:, 1:16:2], T.rr[:, 31:384:48], T.scl[:, 15:16], None, A.mult)
+    fence()
+    V(vec.transpose(T.vt[:, :], T.vv[:, :]))
+    fence()
+    tt(T.v2[:, 0:16], T.vt[:, 0:16], T.vt[:, 16:32], A.add)
+    tt(T.v2[:, 16:32], T.vt[:, 0:16], T.vt[:, 16:32], A.add)
+    fence()
+    V(vec.transpose(T.vb[:, :], T.v2[:, :]))
+    fence()
+    cp(T.offp[:, :], T.vb[:, 0:16])
+    m4 = fence()
+
+    xc = lambda a, b: T.xq[:, 0:128].bitcast(dt.uint32).indirect(T.offp[:, a:b])
+    xz = lambda a, b: T.xz[:, 0:128].indirect(T.offp[:, a:b])
+    vec.tensor_copy(T.oq[:, 32:160].bitcast(dt.uint32), xc(2, 10)).then_inc(sem.pc1, 1)
+    vec.tensor_copy(T.oq[:, 160:256].bitcast(dt.uint32), xc(10, 16)).then_inc(sem.pc2, 1)
+    cp(T.lq[:, 0:32].bitcast(dt.uint32), xc(0, 2))
+    act.wait_ge(sem.v, m4)
+    act.activation(T.oz[:, 32:160], xz(2, 10), Copy).then_inc(sem.pa1, 1)
+    act.activation(T.oz[:, 160:256], xz(10, 16), Copy).then_inc(sem.pa2, 1)
+    S(act.activation(T.lz[:, 0:32], xz(0, 2), Copy))
+
+    g.wait_ge(sem.v, m3)
+    g.wait_ge(sem.n2, 1)
+    send_info(T.info2, T.hand2, T.land2, sem.i2, rs)
+    g.wait_ge(sem.pc1, 1)
+    g.remote_dma_fused([xfer(core, rc[h], topo, half[h], sem.tc, T.oq[:, 32 + 64 * h:96 + 64 * h].bitcast(dt.uint8),
+                             T.rq[:, :].bitcast(dt.uint8)) for h in range(2)], local_sem=sem.lo)
+    g.wait_ge(sem.pa1, 1)
+    g.remote_dma_fused([xfer(core, rs[h], topo, half[h], sem.ts, T.oz[:, 32 + 64 * h:96 + 64 * h],
+                             T.rz[:, :]) for h in range(2)], local_sem=sem.lo)
+    g.wait_ge(sem.pc2, 1)
+    tr = []
+    for i, u in enumerate(direct):
+        b, c = W * ords.index(u), W * slot_of(u)
+        x, y = SPLIT_C[i]
+        tr.append(xfer(core, at(T, topo, s, u), topo, off[x:y], sem.tc, T.oq[:, b:b + W].bitcast(dt.uint8),
+                       T.lq[:, c:c + W].bitcast(dt.uint8)))
+    g.remote_dma_fused(tr, local_sem=sem.lo)
+    g.wait_ge(sem.pa2, 1)
+    tr = []
+    for i, u in enumerate(direct):
+        b, c = W * ords.index(u), W * slot_of(u)
+        x, y = SPLIT_S[i]
+        tr.append(xfer(core, at(T, topo, s, u), topo, off[x:y], sem.ts, T.oz[:, b:b + W], T.lz[:, c:c + W]))
+    g.remote_dma_fused(tr, local_sem=sem.lo)
+    g.wait_ge(sem.lo, 2 * 14 + 2 * 16)
+
+    V(vec.quantize_mx(T.lq[:, LAND:LAND + ROOM], T.lz[:, LAND:LAND + ROOM], T.zt[:, :]))
+    vec.wait_ge(sem.n2, 1)
+    cp(T.land2[:, 0:2], T.info2[:, 0:2])
+    ts(fc(27), K32, 1.0, 32.0, A.is_ge, A.mult)
+    ts(fc(28), K32, 17.0, -32.0, A.is_ge, A.mult)
+    ts(fc(29), K32, 8.0, -256.0, A.is_equal, A.mult)
+    ts(T.jw[:, :], T.jw0[:, :], R16, None, A.add)
+    fence()
+    tt(fc(30), fc(27), fc(28), A.add)
+    fence()
+    tt(T.land2[:, 3:4], fc(30), fc(29), A.add)
+    vec.wait_ge(sem.lw, 16)
+    for o in range(O):
+        V(vec.quantize_mx(T.wq[:, 128 * o:128 * o + 128], T.wz[:, 128 * o:128 * o + 128], T.wt[:, 512 * o:512 * o + 512]))
+    fence()
+
+    vec.wait_ge(sem.i2, n1)
+    V(vec.tensor_reduce(fc(31), T.land2[:, 0:22:2], X, A.add))
+    V(vec.tensor_reduce(fc(32), T.land2[:, 1:22:2], X, A.add))
+    fence()
+    ts(T.st[:, :], T.jd[:, :], fc(31), fc(32), A.is_ge, A.mult)
+    fence()
+    V(vec.transpose(T.stt[:, :], T.st[:, :]))
+    fence()
+    scan(T.sw[:, :], T.kp[:, :], T.stt[:, :], 0.0, A.mult)
+    fence()
+    tt(T.wl[:, :], T.sw[:, 31:320:32], T.jw[:, :], A.add)
+    fence()
+    cp(T.offh[:, :], T.wl[:, :])
+    m5 = fence()
+
+    nt = 0
+    for u in range(1, N):
+        d = order(T, topo, (s - u) % N)[1]
+        nt += SPLIT_C[d.index(u)][1] - SPLIT_C[d.index(u)][0] if u in d else 4
+    act.wait_ge(sem.v, m5)
+    act.wait_ge(sem.a, an[0])
+    act.wait_ge(sem.ts, nt)
+    S(act.activation(T.hz[:, 0:160], T.lz[:, 0:416].indirect(T.offh[:, 0:10]), Copy))
+    a2 = an[0]
+    vec.wait_ge(sem.tc, nt)
+    cp(T.hq[:, 0:160].bitcast(dt.uint32), T.lq[:, 0:416].bitcast(dt.uint32).indirect(T.offh[:, 0:10]))
+    m6 = vn[0]
+    ten.wait_ge(sem.v, m6)
+    ten.wait_ge(sem.a, a2)
+    for o in range(O):
+        ten.matmul_mx(T.ps[:, 512 * o:512 * o + ROOM], T.wq[:, 128 * o:128 * o + 128], T.wz[:, 128 * o:128 * o + 128],
+                      T.hq[:, 0:ROOM], T.hz[:, 0:ROOM], True, True).then_inc(sem["t%d" % o], 1)
+    for o in range(O):
+        y, p = T.ys[:, ROOM * o:ROOM * o + ROOM], T.ps[:, 512 * o:512 * o + ROOM]
+        if o % 2 == 0:
+            vec.wait_ge(sem["t%d" % o], 1)
+            vec.tensor_copy(y, p).then_inc(sem["y%d" % o], 1)
+        else:
+            act.wait_ge(sem["t%d" % o], 1)
+            act.activation(y, p, Copy).then_inc(sem["y%d" % o], 1)
+    for q, o in ((g.sync, 0), (act, 2)):
+        q.wait_ge(sem["y%d" % o], 1)
+        q.wait_ge(sem["y%d" % (o + 1)], 1)
+        q.dma_start(T.y[:, ROOM * o:ROOM * o + 2 * ROOM], T.ys[:, ROOM * o:ROOM * o + 2 * ROOM]).then_inc(sem.ly, 16)
+    act.wait_ge(sem.ly, 32)

@@ -10,14 +10,14 @@ LAND = N * W
 F4, B2, I4, U2, MX, U1 = "float32", "bfloat16", "int32", "uint16", "float8_e4m3fn_x4", "uint8"
 SIZES = {
     I4: dict(c1b=8, c2b=8, cm=8, cs=8, pi=1, kk=8, r1i=64, r2i=64, r1=64, r2=64),
-    U2: dict(cu=8, so=4, offp=16, offh=10),
-    F4: dict(kf=8, bo=32, bt=32, ic=32, k32=320, kp=320, x16=384, kr=384, jd=320, jw0=10, jw=10, val0=64, val=64,
-             sc0=16, sc1=16, scl=16, fc=48, cr=96, c2c=64, cda=32, cdb=32, ca=128, cb=128, ya1=128, yb1=128, ya=128, yb=128,
-             e1=96, e1t=96, e2=64, e2t=64, e2s=8, cum=128, mm=128, mt=128, ss=128, win=384, rr=384, vv=32, vt=32, v2=32,
-             vb=32, st=320, stt=320, sw=320, wl=10, ys=640),
-    B2: dict(tn=64, ta=64, tb=64, te=64, tia=64, tib=64, eq2=64, eqa=64, eqb=64, gn=128, ga=128, gb=128, ge=128, gia=128,
-             gib=128, xa=128, xb=128, xs=128,
-             info1=16, info2=16, hand1=4, hand2=4, land1=22, land2=22,
+    U2: dict(cu=8, cu1=8, so=4, offp=16, offh=10),
+    F4: dict(kf=8, bo=32, bt=32, wr=32, wc=32, ic=32, jw0=10, jw=10, val0=64, val=64, sc0=16, sc1=16, scl=16, fc=48,
+             cum=128, mm=128, mt=128, ss=128, win=384, rr=384, vv=32, vt=32, v2=32, vb=32, sw=320, wl=10, ys=640),
+    B2: dict(cr=96, c2c=64, cda=32, cdb=32, ca=128, cb=128, ya1=128, yb1=128, e1=96, e1t=96, e2=64, e2t=64, e2s=8,
+             k32=320, x16=384, kr=384, kp=320, jd=320, st=320, stt=320,
+             tn=8, ta=64, tb=64, te=64, tia=64, tib=64, eq2=64, eqa=64, eqb=64, gn=128, ga=128, gb=128, ge=128, gia=128,
+             gib=128, ya=128, yb=128, xa=128, xb=128, xs=128,
+             info1=16, info2=16, hand1=2, hand2=4, land1=22, land2=22,
              xt=512, wt=2048, zt=640),
     MX: dict(xq=128, wq=512, oq=256, rq=64, lq=416, hq=160),
     U1: dict(xz=128, wz=512, oz=256, rz=64, lz=416, hz=160),
@@ -26,7 +26,7 @@ SCRATCH = {"ps": ("psum", [128, 2048], F4)}
 for _d in SIZES:
     for _n in SIZES[_d]:
         SCRATCH[_n] = ("sbuf", [128, SIZES[_d][_n]], _d)
-SEMAPHORES = ["v", "a", "p", "ld", "lx", "lw", "ly", "i1", "i2", "tc", "ts", "lo", "pc1", "pc2", "pa1", "pa2", "n2",
+SEMAPHORES = ["v", "a", "p", "ld", "le", "lx", "lw", "ly", "i1", "i2", "tc", "ts", "lo", "pc1", "pc2", "pa1", "pa2", "n2",
               "t0", "t1", "t2", "t3", "y0", "y1", "y2", "y3"]
 
 
@@ -74,33 +74,35 @@ def hand_on(g, core, T, topo):
     for s in range(N):
         cross, _ = order(T, topo, s)
         rc, rs = relays(T, topo, s)
-        for h in range(2):
-            us = cross[2 * h:2 * h + 2]
-            for kind, who in (("c", rc), ("s", rs)):
-                if who[h] != core:
-                    continue
-                es = [topo.engines(core, at(T, topo, s, u)) for u in us]
-                es = [es[0][0:4], es[1][4:8]]
-                isem, tsem = (T.sem.i1, T.sem.tc) if kind == "c" else (T.sem.i2, T.sem.ts)
-                hand, land = (T.hand1, T.land1) if kind == "c" else (T.hand2, T.land2)
-                g.wait_ge(isem, 4)
-                tr = []
-                for i, u in enumerate(us):
-                    c = 8 + 2 * (slot_of(u) - 1)
-                    tr.append(xfer(core, at(T, topo, s, u), topo, es[i], isem, hand[:, 2 * i:2 * i + 2], land[:, c:c + 2]))
-                g.remote_dma_fused(tr, local_sem=T.sem.lo)
-                g.wait_ge(tsem, 4)
-                tr = []
-                for i, u in enumerate(us):
-                    c = W * slot_of(u)
-                    if kind == "c":
-                        a, b = T.rq[:, W * i:W * i + W].bitcast(dt.uint8), T.lq[:, c:c + W].bitcast(dt.uint8)
-                    else:
-                        a, b = T.rz[:, W * i:W * i + W], T.lz[:, c:c + W]
-                    tr.append(xfer(core, at(T, topo, s, u), topo, es[i], tsem, a, b))
-                g.remote_dma_fused(tr, local_sem=T.sem.lo)
-                g.wait_ge(T.sem.lo, 16)
-                return
+        if core not in rc + rs:
+            continue
+        codes = core in rc
+        h = (rc if codes else rs).index(core)
+        us = cross[2 * h:2 * h + 2]
+        dst = [at(T, topo, s, u) for u in us]
+        es = [topo.engines(core, d) for d in dst]
+        col = [8 + 2 * (slot_of(u) - 1) for u in us]
+        j = 0 if codes else 1
+        g.wait_ge(T.sem.i1, 4)
+        g.remote_dma_fused([xfer(core, dst[j], topo, es[j], T.sem.i1, T.hand1[:, :], T.land1[:, col[j]:col[j] + 2])],
+                           local_sem=T.sem.lo)
+        es = [es[0][0:4], es[1][4:8]]
+        if codes:
+            g.wait_ge(T.sem.i2, 4)
+            g.remote_dma_fused([xfer(core, dst[i], topo, es[i], T.sem.i2, T.hand2[:, 2 * i:2 * i + 2],
+                                     T.land2[:, col[i]:col[i] + 2]) for i in range(2)], local_sem=T.sem.lo)
+        tr = []
+        for i, u in enumerate(us):
+            c = W * slot_of(u)
+            if codes:
+                a, b = T.rq[:, W * i:W * i + W].bitcast(dt.uint8), T.lq[:, c:c + W].bitcast(dt.uint8)
+            else:
+                a, b = T.rz[:, W * i:W * i + W], T.lz[:, c:c + W]
+            tr.append(xfer(core, dst[i], topo, es[i], T.sem.tc if codes else T.sem.ts, a, b))
+        g.wait_ge(T.sem.tc if codes else T.sem.ts, 8 if codes else 4)
+        g.remote_dma_fused(tr, local_sem=T.sem.lo)
+        g.wait_ge(T.sem.lo, 24 if codes else 16)
+        return
 
 
 def rank_program(g, core, T, topo):
@@ -109,7 +111,7 @@ def rank_program(g, core, T, topo):
         hand_on(g, core, T, topo)
         return
     A, X = AluOpType, AxisListType.X
-    Copy = ActivationFunctionType.Copy
+    Copy, Ident = ActivationFunctionType.Copy, ActivationFunctionType.Identity
     sem = T.sem
     vec, act, ten = g.vector, g.scalar, g.tensor
     cross, direct = order(T, topo, s)
@@ -161,11 +163,13 @@ def rank_program(g, core, T, topo):
             g.iota(out, pattern, base, cm).then_inc(sem.p, 1)
         pn[0] += 1
 
-    for q in range(8):
-        g.sync.dma_start(T.c1b[16 * q:16 * q + 16, :], T.c1[:, :]).then_inc(sem.ld, 16)
-        act.dma_start(T.c2b[16 * q:16 * q + 16, :], T.c2[:, :]).then_inc(sem.ld, 16)
+    for big, src, sm in ((T.c1b, T.c1, sem.ld), (T.c2b, T.c2, sem.le)):
+        for q in range(8):
+            dq = g.sync if q % 2 else act
+            dq.dma_start(big[16 * q:16 * q + 16, :], src[:, :]).then_inc(sm, 16)
     g.sync.dma_start(T.xt[:, :], T.x[:, :]).then_inc(sem.lx, 16)
 
+    I(T.ic[:, :], [[1, 32]], 0)
     I(T.pi[:, :], [[0, 1]], 0, 1, False)
     k = 0
     while k < N:
@@ -184,43 +188,26 @@ def rank_program(g, core, T, topo):
     UO = T.bt[:, 0:1]
     k1, k2 = ords.index(1), ords.index(2)
 
+    fill(T.wr[:, :], 0.0)
     fill(T.cr[:, :], 0.0)
     fence()
+    for i in range(N):
+        fill(T.wr[:, i:i + 1], (s + ords[i] + 1) % N)
+        fill(T.wr[:, 8 + i:9 + i], (s + ords[i] + 2) % N if ords[i] + 1 < N else N)
+    fence()
+    V(vec.transpose(T.wc[:, :], T.wr[:, :]))
     fill(T.cr[:, k1:k1 + 1], 1.0)
     fill(T.cr[:, 8:16], -1.0)
     fill(T.cr[:, 32 + k2:33 + k2], 1.0)
     fill(T.cr[:, 72:80], -1.0)
-    vec.wait_ge(sem.p, p1)
-    ts(T.kk[:, 0:1], T.pi[:, :], 7, None, A.bitwise_and)
-    ts(T.kk[:, 1:2], T.pi[:, :], 3, 3, A.logical_shift_right, A.bitwise_and)
-    ts(T.kk[:, 2:3], T.pi[:, :], 31, None, A.bitwise_and)
-    ts(T.kk[:, 3:4], T.pi[:, :], 15, None, A.bitwise_and)
-    ts(T.kk[:, 4:5], T.pi[:, :], 4, 1, A.logical_shift_right, A.bitwise_and)
-    ts(T.r1[:, :], T.r1i[:, :], 7, None, A.bitwise_and)
-    ts(T.r2[:, :], T.r2i[:, :], 7, None, A.bitwise_and)
-    cp(T.bo[:, 8:16], T.bo[:, 0:8])
     fence()
-    cp(T.kf[:, 0:5], T.kk[:, 0:5])
-    cp(T.bo[:, 16:32], T.bo[:, 0:16])
-    fence()
-    V(vec.transpose(T.bt[:, :], T.bo[:, :]))
-    fence()
-    ts(fc(0), TY, 1.0, UO, A.add, A.add)
-    fence()
-    ts(fc(1), fc(0), 8.0, -8.0, A.is_equal, A.mult)
-    fence()
-    tt(fc(2), fc(0), fc(1), A.add)
-    fence()
-    ts(T.tn[:, :], T.r1[:, :], fc(2), None, A.is_equal)
+    vec.wait_ge(sem.p, 1)
+    ts(T.tn[:, :], T.ic[:, 0:8], T.wc[:, 0:1], None, A.is_equal)
 
-    vec.wait_ge(sem.ld, 256)
-    ts(T.cm[:, :], T.c1b[:, :], 8, None, A.mult)
+    vec.wait_ge(sem.ld, 128)
+    cp(T.cu1[:, :], T.c1b[:, :])
     fence()
-    tt(T.cs[:, :], T.cm[:, :], T.c2b[:, :], A.add)
-    fence()
-    cp(T.cu[:, :], T.cs[:, :])
-    fence()
-    cp(T.gn[:, :], T.tn[:, 0:64].indirect(T.cu[:, 0:8]))
+    cp(T.gn[:, :], T.tn[:, 0:8].indirect(T.cu1[:, 0:8]))
     fence()
     V(vec.tensor_reduce(fc(3), T.gn[:, :], X, A.add))
     fence()
@@ -235,58 +222,79 @@ def rank_program(g, core, T, topo):
     off = topo.engines(core, at(T, topo, s, direct[0]))
     on = [e for e in topo.engines(core, rc[0]) if e not in off]
     half = [on[0:4], on[4:8]]
+    grp = [off[0:4], off[4:8]] + half
+    to = [rc[0], rs[0], rc[1], rs[1]]
 
-    def send_info(info, hand, land, isem, who):
-        tr = [xfer(core, who[h], topo, half[h], isem, info[:, 2 + 4 * h:6 + 4 * h], hand[:, :]) for h in range(2)]
-        g.remote_dma_fused(tr, local_sem=sem.lo)
+    def to_plane(info, land, isem):
         tr = []
         for i, u in enumerate(direct):
-            b = 2 * ords.index(u)
-            c = 8 + 2 * (slot_of(u) - 1)
+            b, c = 2 * ords.index(u), 8 + 2 * (slot_of(u) - 1)
             tr.append(xfer(core, at(T, topo, s, u), topo, off[2 * i:2 * i + 2], isem, info[:, b:b + 2], land[:, c:c + 2]))
         g.remote_dma_fused(tr, local_sem=sem.lo)
 
-    I(T.ic[:, :], [[1, 32]], 0)
-    I(T.x16[:, :], [[0, 24], [1, 16]], 0)
     g.wait_ge(sem.v, m1)
-    send_info(T.info1, T.hand1, T.land1, sem.i1, rc)
+    g.remote_dma_fused([xfer(core, to[j], topo, grp[j], sem.i1, T.info1[:, 2 + 2 * j:4 + 2 * j], T.hand1[:, :])
+                        for j in range(4)], local_sem=sem.lo)
+    to_plane(T.info1, T.land1, sem.i1)
+    I(T.x16[:, :], [[0, 24], [1, 16]], 0)
+    px = pn[0]
     I(T.k32[:, :], [[0, 10], [1, 32]], 0)
     I(T.val0[:, :], [[32, 4], [1, 16]], 0)
     I(T.jw0[:, :], [[16, 10]], 0)
-    I(T.jd[:, :], [[16, 10], [0, 2], [1, 16]], 0)
     p2 = pn[0]
+    I(T.jd[:, :], [[16, 10], [0, 2], [1, 16]], 0)
+    p3 = pn[0]
 
     ISS, ISF, ISN = fc(4), fc(5), fc(6)
+    vec.wait_ge(sem.p, p1)
+    cp(T.bo[:, 8:16], T.bo[:, 0:8])
+    ts(T.kk[:, 0:1], T.pi[:, :], 7, None, A.bitwise_and)
+    ts(T.kk[:, 1:2], T.pi[:, :], 3, 3, A.logical_shift_right, A.bitwise_and)
+    ts(T.kk[:, 2:3], T.pi[:, :], 31, None, A.bitwise_and)
+    ts(T.kk[:, 3:4], T.pi[:, :], 15, None, A.bitwise_and)
+    ts(T.kk[:, 4:5], T.pi[:, :], 4, 1, A.logical_shift_right, A.bitwise_and)
+    ts(T.r1[:, :], T.r1i[:, :], 7, None, A.bitwise_and)
+    ts(T.r2[:, :], T.r2i[:, :], 7, None, A.bitwise_and)
+    vec.wait_ge(sem.le, 128)
+    ts(T.cm[:, :], T.c1b[:, :], 8, None, A.mult)
+    fence()
+    cp(T.bo[:, 16:32], T.bo[:, 0:16])
+    cp(T.kf[:, 0:5], T.kk[:, 0:5])
+    tt(T.cs[:, :], T.cm[:, :], T.c2b[:, :], A.add)
+    fence()
+    V(vec.transpose(T.bt[:, :], T.bo[:, :]))
     ts(ISS, TY, 1.0, None, A.is_equal)
     ts(ISF, TY, 0.0, None, A.is_equal)
     ts(ISN, TY, 2.0, None, A.is_equal)
+    ts(T.tb[:, :], T.r1[:, :], 2.0, None, A.is_equal)
+    fence()
     ts(fc(7), UO, -1.0, 1.0, A.mult, A.add)
     ts(T.te[:, :], T.r1[:, :], UO, None, A.is_equal)
-    ts(T.tb[:, :], T.r1[:, :], 2.0, None, A.is_equal)
     ts(T.eq2[:, :], T.r2[:, :], UO, None, A.is_equal)
+    ts(fc(9), ISS, -1.0, 1.0, A.mult, A.add)
     fence()
     ts(fc(8), fc(7), ISS, UO, A.mult, A.add)
-    ts(fc(9), ISS, -1.0, 1.0, A.mult, A.add)
+    cp(T.cu[:, :], T.cs[:, :])
     ts(T.eqb[:, :], T.eq2[:, :], ISS, None, A.mult)
+    ts(T.eqa[:, :], T.eq2[:, :], fc(9), None, A.max)
     fence()
     ts(T.ta[:, :], T.r1[:, :], fc(8), None, A.is_equal)
-    ts(T.eqa[:, :], T.eq2[:, :], fc(9), None, A.max)
     tt(T.tib[:, :], T.tb[:, :], T.eqb[:, :], A.mult)
     fence()
     tt(T.tia[:, :], T.ta[:, :], T.eqa[:, :], A.mult)
     m2 = fence()
 
+    act.wait_ge(sem.p, px)
+    S(act.activation(T.win[:, :], T.x16[:, :], Copy, scale=0.0))
+    S(act.activation(T.vv[:, :], T.x16[:, 0:32], Copy, scale=0.0))
     act.wait_ge(sem.v, m2)
     for out, tab in ((T.ga, T.ta), (T.gb, T.tb), (T.gia, T.tia), (T.gib, T.tib), (T.ge, T.te)):
         S(act.activation(out[:, :], tab[:, 0:64].indirect(T.cu[:, 0:8]), Copy))
     a1 = an[0]
     act.dma_start(T.wt[:, :], T.w[:, :]).then_inc(sem.lw, 16)
 
-    fill(T.zt[:, :], 0.0)
+    fill(T.zt[:, 0:128], 0.0)
     fill(T.land1[:, 0:8], 0.0)
-    fill(T.land2[:, 0:8], 0.0)
-    fill(T.win[:, :], 0.0)
-    fill(T.vv[:, :], 0.0)
     tt(fc(10), ISS, ISF, A.subtract)
     ts(fc(11), TY, -64.0, 174.0, A.mult, A.add)
     ts(fc(12), KAP8, 48.0, -1.0, A.mult, A.add)
@@ -316,11 +324,12 @@ def rank_program(g, core, T, topo):
     tt(T.ya[:, :], T.ya1[:, :], T.gia[:, :], A.mult)
     tt(T.yb[:, :], T.yb1[:, :], T.gib[:, :], A.mult)
     BASE = fc(23)
+    ts(fc(33), BASE, -1.0, None, A.mult)
     vec.wait_ge(sem.p, p2)
     ts(T.c2c[:, 0:32], T.ic[:, :], fc(17), None, A.is_gt)
     ts(T.cda[:, :], T.ic[:, :], fc(20), None, A.is_equal)
     ts(T.cdb[:, :], T.ic[:, :], fc(21), None, A.is_equal)
-    ts(T.kp[:, :], T.k32[:, :], 1.0, None, A.min)
+    ts(T.kp[:, 0:128], T.k32[:, 0:128], 1.0, None, A.min)
     ts(T.kr[:, :], T.x16[:, :], R16, 256.0, A.is_gt, A.mult)
     ts(T.sc0[:, :], T.x16[:, 0:16], R16, 1.0 / 256.0, A.is_gt, A.mult)
     ts(T.sc1[:, :], T.x16[:, 0:16], R16, None, A.is_equal)
@@ -332,9 +341,11 @@ def rank_program(g, core, T, topo):
     V(vec.quantize_mx(T.xq[:, 0:128], T.xz[:, 0:128], T.xt[:, :]))
     fence()
 
-    n1 = 0
+    n1 = n2 = 0
     for u in range(1, N):
-        n1 += 2 if u in order(T, topo, (s - u) % N)[1] else 4
+        here = u in order(T, topo, (s - u) % N)[1]
+        n1 += 2 if here else 8
+        n2 += 2 if here else 4
     vec.wait_ge(sem.i1, n1)
     V(vec.tensor_reduce(fc(24), T.land1[:, 0:22:2], X, A.add))
     V(vec.tensor_reduce(fc(25), T.land1[:, 1:22:2], X, A.add))
@@ -344,19 +355,22 @@ def rank_program(g, core, T, topo):
     fence()
     scan(T.cum[:, :], T.xa[:, :], T.xb[:, :], BASE, A.add)
     tt(T.xs[:, :], T.xa[:, :], T.xb[:, :], A.add)
-    fence()
-    ts(fc(26), T.cum[:, 127:128], BASE, None, A.subtract)
+    mc = fence()
+    act.wait_ge(sem.v, mc)
+    S(act.activation(fc(26), T.cum[:, 127:128], Ident, bias=fc(33)))
+    act.wait_ge(sem.a, an[0])
+    S(act.activation(T.e2[:, :], T.c2c[:, :], Copy, scale=fc(26)))
     tt(T.mm[:, :], T.xs[:, :], T.cum[:, :], A.mult)
     fence()
-    ts(T.e2[:, :], T.c2c[:, :], fc(26), None, A.mult)
     V(vec.transpose(T.mt[:, :], T.mm[:, :]))
     fence()
-    V(vec.transpose(T.e2t[:, :], T.e2[:, :]))
     scan(T.ss[:, :], T.kp[:, 0:128], T.mt[:, :], 0.0, A.mult)
+    vec.wait_ge(sem.a, an[0])
+    V(vec.transpose(T.e2t[:, :], T.e2[:, :]))
     fence()
+    cp(T.so[:, :], T.ss[:, 15:128:32])
     tt(T.info2[:, 0:16:2], T.e2t[:, 0:8], T.e2t[:, 8:16], A.add)
     tt(T.e2s[:, :], T.e2t[:, 32:40], T.e2t[:, 40:48], A.add)
-    cp(T.so[:, :], T.ss[:, 15:128:32])
     m3 = fence()
     vec.tensor_tensor(T.info2[:, 1:16:2], T.e2s[:, :], T.e2t[:, 48:56], A.add).then_inc(sem.n2, 1)
     cp(T.win[:, 0:384].indirect(T.so[:, 0:4]), T.val[:, :])
@@ -388,9 +402,11 @@ def rank_program(g, core, T, topo):
 
     g.wait_ge(sem.v, m3)
     g.wait_ge(sem.n2, 1)
-    send_info(T.info2, T.hand2, T.land2, sem.i2, rs)
+    g.remote_dma_fused([xfer(core, rc[h], topo, half[h], sem.i2, T.info2[:, 2 + 4 * h:6 + 4 * h], T.hand2[:, :])
+                        for h in range(2)], local_sem=sem.lo)
+    to_plane(T.info2, T.land2, sem.i2)
     g.wait_ge(sem.pc1, 1)
-    g.remote_dma_fused([xfer(core, rc[h], topo, half[h], sem.tc, T.oq[:, 32 + 64 * h:96 + 64 * h].bitcast(dt.uint8),
+    g.remote_dma_fused([xfer(core, rc[h], topo, (off, on)[h], sem.tc, T.oq[:, 32 + 64 * h:96 + 64 * h].bitcast(dt.uint8),
                              T.rq[:, :].bitcast(dt.uint8)) for h in range(2)], local_sem=sem.lo)
     g.wait_ge(sem.pa1, 1)
     g.remote_dma_fused([xfer(core, rs[h], topo, half[h], sem.ts, T.oz[:, 32 + 64 * h:96 + 64 * h],
@@ -410,8 +426,12 @@ def rank_program(g, core, T, topo):
         x, y = SPLIT_S[i]
         tr.append(xfer(core, at(T, topo, s, u), topo, off[x:y], sem.ts, T.oz[:, b:b + W], T.lz[:, c:c + W]))
     g.remote_dma_fused(tr, local_sem=sem.lo)
-    g.wait_ge(sem.lo, 2 * 14 + 2 * 16)
+    g.wait_ge(sem.lo, 22 + 14 + 16 + 3 * 8)
 
+    fill(T.zt[:, 128:640], 0.0)
+    fill(T.land2[:, 0:8], 0.0)
+    ts(T.kp[:, 128:320], T.k32[:, 128:320], 1.0, None, A.min)
+    fence()
     V(vec.quantize_mx(T.lq[:, LAND:LAND + ROOM], T.lz[:, LAND:LAND + ROOM], T.zt[:, :]))
     vec.wait_ge(sem.n2, 1)
     cp(T.land2[:, 0:2], T.info2[:, 0:2])
@@ -428,7 +448,8 @@ def rank_program(g, core, T, topo):
         V(vec.quantize_mx(T.wq[:, 128 * o:128 * o + 128], T.wz[:, 128 * o:128 * o + 128], T.wt[:, 512 * o:512 * o + 512]))
     fence()
 
-    vec.wait_ge(sem.i2, n1)
+    vec.wait_ge(sem.p, p3)
+    vec.wait_ge(sem.i2, n2)
     V(vec.tensor_reduce(fc(31), T.land2[:, 0:22:2], X, A.add))
     V(vec.tensor_reduce(fc(32), T.land2[:, 1:22:2], X, A.add))
     fence()
@@ -468,8 +489,8 @@ def rank_program(g, core, T, topo):
         else:
             act.wait_ge(sem["t%d" % o], 1)
             act.activation(y, p, Copy).then_inc(sem["y%d" % o], 1)
-    for q, o in ((g.sync, 0), (act, 2)):
-        q.wait_ge(sem["y%d" % o], 1)
-        q.wait_ge(sem["y%d" % (o + 1)], 1)
-        q.dma_start(T.y[:, ROOM * o:ROOM * o + 2 * ROOM], T.ys[:, ROOM * o:ROOM * o + 2 * ROOM]).then_inc(sem.ly, 16)
+    for q, o, e in ((g.sync, 0, 1), (act, 1, 4)):
+        for k in range(o, e):
+            q.wait_ge(sem["y%d" % k], 1)
+        q.dma_start(T.y[:, ROOM * o:ROOM * e], T.ys[:, ROOM * o:ROOM * e]).then_inc(sem.ly, 16)
     act.wait_ge(sem.ly, 32)

import numpy as np
from concourse.bass import DstId, RemoteDMATransfer
from concourse.mybir import dt, AluOpType, AxisListType, ActivationFunctionType

N = 8
CAP, ROOM, O = 144, 160, 4
W = 32
LAND = N * W

F4, B2, I4, U2, MX, U1 = "float32", "bfloat16", "int32", "uint16", "float8_e4m3fn_x4", "uint8"
SIZES = {
    I4: dict(c1b=8, c2b=8, cm=8, cs=8, pi=1, kk=8, r1i=64, r2i=64, r1=64, r2=64),
    U2: dict(cu=8, cu1=8, so=4, offp=16, offh=10),
    F4: dict(kf=8, bo=32, bt=32, wr=32, wc=32, ic=32, jw0=10, jw=10, val0=64, val=64, sc0=16, sc1=16, scl=16, fc=48,
             cum=128, mm=128, mt=128, ss=128, win=384, rr=384, vv=32, vt=32, v2=32, vb=32, sw=320, wl=10, ys=640),
    B2: dict(cr=96, c2c=64, cda=32, cdb=32, ca=128, cb=128, ya1=128, yb1=128, e1=96, e1t=96, e2=64, e2t=64, e2s=8,
             k32=320, x16=384, kr=384, kp=320, jd=320, st=320, stt=320,
             tn=8, ta=64, tb=64, te=64, tia=64, tib=64, eq2=64, eqa=64, eqb=64, gn=128, ga=128, gb=128, ge=128, gia=128,
             gib=128, ya=128, yb=128, xa=128, xb=128, xs=128,
             info1=16, info2=16, hand1=2, hand2=4, land1=22, land2=22,
             xt=512, wt=2048, zt=640),
    MX: dict(xq=128, wq=512, oq=256, rq=64, lq=416, hq=160),
    U1: dict(xz=128, wz=512, oz=256, rz=64, lz=416, hz=160),
}
SCRATCH = {"ps": ("psum", [128, 2048], F4)}
for _d in SIZES:
    for _n in SIZES[_d]:
        SCRATCH[_n] = ("sbuf", [128, SIZES[_d][_n]], _d)
SEMAPHORES = ["v", "a", "p", "ld", "le", "lx", "lw", "ly", "i1", "i2", "tc", "ts", "lo", "pc1", "pc2", "pa1", "pa2", "n2",
              "t0", "t1", "t2", "t3", "y0", "y1", "y2", "y3"]


def bits(es):
    m = 0
    for e in es:
        m |= 1 << e
    return m


def at(T, topo, s, u):
    return T.cores[(s + u) % N]


def order(T, topo, s):
    cross = [u for u in range(1, N) if not topo.may_write(T.cores[s], at(T, topo, s, u))]
    direct = [u for u in range(1, N) if u not in cross]
    return cross, direct


def relays(T, topo, s):
    me = T.cores[s]
    cross, _ = order(T, topo, s)
    r = [c for c in topo.cores_of(me) if c != me and T.rank_of(c) is None
         and all(topo.may_write(c, at(T, topo, s, u)) for u in cross)]
    near = [c for c in r if topo.die(c) == topo.die(me)]
    far = [c for c in r if topo.die(c) != topo.die(me)]
    return [near[0], far[0]], [far[1], near[1]]


SPLIT_C = ((0, 2), (2, 4), (4, 8))
SPLIT_S = ((4, 6), (6, 8), (0, 4))


def xfer(core, d, topo, es, sem, src, dst):
    rid, pid = topo.addr(d, core)
    return RemoteDMATransfer(dst_ids=[DstId(rid=rid, pnc=pid)], dma_engine_mask=bits(es), remote_sem=sem, src=src, dst=dst)


def slot_of(u):
    return (N - u) % N


def hand_on(g, core, T, topo):
    for s in range(N):
        cross, _ = order(T, topo, s)
        rc, rs = relays(T, topo, s)
        if core not in rc + rs:
            continue
        codes = core in rc
        h = (rc if codes else rs).index(core)
        us = cross[2 * h:2 * h + 2]
        dst = [at(T, topo, s, u) for u in us]
        es = [topo.engines(core, d) for d in dst]
        col = [8 + 2 * (slot_of(u) - 1) for u in us]
        j = 0 if codes else 1
        g.wait_ge(T.sem.i1, 4)
        g.remote_dma_fused([xfer(core, dst[j], topo, es[j], T.sem.i1, T.hand1[:, :], T.land1[:, col[j]:col[j] + 2])],
                           local_sem=T.sem.lo)
        es = [es[0][0:4], es[1][4:8]]
        if codes:
            g.wait_ge(T.sem.i2, 4)
            g.remote_dma_fused([xfer(core, dst[i], topo, es[i], T.sem.i2, T.hand2[:, 2 * i:2 * i + 2],
                                     T.land2[:, col[i]:col[i] + 2]) for i in range(2)], local_sem=T.sem.lo)
        tr = []
        for i, u in enumerate(us):
            c = W * slot_of(u)
            if codes:
                a, b = T.rq[:, W * i:W * i + W].bitcast(dt.uint8), T.lq[:, c:c + W].bitcast(dt.uint8)
            else:
                a, b = T.rz[:, W * i:W * i + W], T.lz[:, c:c + W]
            tr.append(xfer(core, dst[i], topo, es[i], T.sem.tc if codes else T.sem.ts, a, b))
        g.wait_ge(T.sem.tc if codes else T.sem.ts, 8 if codes else 4)
        g.remote_dma_fused(tr, local_sem=T.sem.lo)
        g.wait_ge(T.sem.lo, 24 if codes else 16)
        return


def rank_program(g, core, T, topo):
    s = T.rank_of(core)
    if s is None:
        hand_on(g, core, T, topo)
        return
    A, X = AluOpType, AxisListType.X
    Copy, Ident = ActivationFunctionType.Copy, ActivationFunctionType.Identity
    sem = T.sem
    vec, act, ten = g.vector, g.scalar, g.tensor
    cross, direct = order(T, topo, s)
    ords = [0] + cross + direct
    rc, rs = relays(T, topo, s)

    vn, vw = [0], [0]

    def V(ins):
        ins.then_inc(sem.v, 1)
        vn[0] += 1

    def fence():
        if vw[0] < vn[0]:
            vec.wait_ge(sem.v, vn[0])
            vw[0] = vn[0]
        return vn[0]

    def ts(out, in0, a, b, op0, op1=None):
        if op1 is None:
            V(vec.tensor_scalar(out, in0, a, None, op0))
        else:
            V(vec.tensor_scalar(out, in0, a, b, op0, op1))

    def tt(out, a, b, op):
        V(vec.tensor_tensor(out, a, b, op))

    def cp(out, a):
        V(vec.tensor_copy(out, a))

    def fill(out, c):
        V(vec.memset(out, c))

    def scan(out, a, b, ini, op0):
        V(vec.tensor_tensor_scan(out, a, b, ini, op0, A.add))

    an = [0]

    def S(ins):
        ins.then_inc(sem.a, 1)
        an[0] += 1

    pn = [0]

    def I(out, pattern, base, cm=0, f=True):
        if f:
            g.iota(out, pattern, base, cm, allow_small_or_imprecise_dtypes=True).then_inc(sem.p, 1)
        else:
            g.iota(out, pattern, base, cm).then_inc(sem.p, 1)
        pn[0] += 1

    for big, src, sm in ((T.c1b, T.c1, sem.ld), (T.c2b, T.c2, sem.le)):
        for q in range(8):
            dq = g.sync if q % 2 else act
            dq.dma_start(big[16 * q:16 * q + 16, :], src[:, :]).then_inc(sm, 16)
    g.sync.dma_start(T.xt[:, :], T.x[:, :]).then_inc(sem.lx, 16)

    I(T.ic[:, :], [[1, 32]], 0)
    I(T.pi[:, :], [[0, 1]], 0, 1, False)
    k = 0
    while k < N:
        n = 1
        step = ords[k + 1] - ords[k] if k + 1 < N else 0
        while k + n < N and ords[k + n] - ords[k + n - 1] == step:
            n += 1
        I(T.bo[:, k:k + n], [[step, n]], ords[k])
        k += n
    I(T.r1i[:, :], [[1, 8], [0, 8]], 8 - s, 0, False)
    I(T.r2i[:, :], [[0, 8], [1, 8]], 8 - s, 0, False)
    p1 = pn[0]

    fc = lambda i: T.fc[:, i:i + 1]
    KAP8, TY, K32, R16, HALF = [T.kf[:, i:i + 1] for i in range(5)]
    UO = T.bt[:, 0:1]
    k1, k2 = ords.index(1), ords.index(2)

    fill(T.wr[:, :], 0.0)
    fill(T.cr[:, :], 0.0)
    fence()
    for i in range(N):
        fill(T.wr[:, i:i + 1], (s + ords[i] + 1) % N)
        fill(T.wr[:, 8 + i:9 + i], (s + ords[i] + 2) % N if ords[i] + 1 < N else N)
    fence()
    V(vec.transpose(T.wc[:, :], T.wr[:, :]))
    fill(T.cr[:, k1:k1 + 1], 1.0)
    fill(T.cr[:, 8:16], -1.0)
    fill(T.cr[:, 32 + k2:33 + k2], 1.0)
    fill(T.cr[:, 72:80], -1.0)
    fence()
    vec.wait_ge(sem.p, 1)
    ts(T.tn[:, :], T.ic[:, 0:8], T.wc[:, 0:1], None, A.is_equal)

    vec.wait_ge(sem.ld, 128)
    cp(T.cu1[:, :], T.c1b[:, :])
    fence()
    cp(T.gn[:, :], T.tn[:, 0:8].indirect(T.cu1[:, 0:8]))
    fence()
    V(vec.tensor_reduce(fc(3), T.gn[:, :], X, A.add))
    fence()
    ts(T.e1[:, :], T.cr[:, :], fc(3), None, A.mult)
    fence()
    V(vec.transpose(T.e1t[:, :], T.e1[:, :]))
    fence()
    tt(T.info1[:, 0:16:2], T.e1t[:, 0:8], T.e1t[:, 40:48], A.add)
    cp(T.info1[:, 1:16:2], T.e1t[:, 72:80])
    m1 = fence()

    off = topo.engines(core, at(T, topo, s, direct[0]))
    on = [e for e in topo.engines(core, rc[0]) if e not in off]
    half = [on[0:4], on[4:8]]
    grp = [off[0:4], off[4:8]] + half
    to = [rc[0], rs[0], rc[1], rs[1]]

    def to_plane(info, land, isem):
        tr = []
        for i, u in enumerate(direct):
            b, c = 2 * ords.index(u), 8 + 2 * (slot_of(u) - 1)
            tr.append(xfer(core, at(T, topo, s, u), topo, off[2 * i:2 * i + 2], isem, info[:, b:b + 2], land[:, c:c + 2]))
        g.remote_dma_fused(tr, local_sem=sem.lo)

    g.wait_ge(sem.v, m1)
    g.remote_dma_fused([xfer(core, to[j], topo, grp[j], sem.i1, T.info1[:, 2 + 2 * j:4 + 2 * j], T.hand1[:, :])
                        for j in range(4)], local_sem=sem.lo)
    to_plane(T.info1, T.land1, sem.i1)
    I(T.x16[:, :], [[0, 24], [1, 16]], 0)
    px = pn[0]
    I(T.k32[:, :], [[0, 10], [1, 32]], 0)
    I(T.val0[:, :], [[32, 4], [1, 16]], 0)
    I(T.jw0[:, :], [[16, 10]], 0)
    p2 = pn[0]
    I(T.jd[:, :], [[16, 10], [0, 2], [1, 16]], 0)
    p3 = pn[0]

    ISS, ISF, ISN = fc(4), fc(5), fc(6)
    vec.wait_ge(sem.p, p1)
    cp(T.bo[:, 8:16], T.bo[:, 0:8])
    ts(T.kk[:, 0:1], T.pi[:, :], 7, None, A.bitwise_and)
    ts(T.kk[:, 1:2], T.pi[:, :], 3, 3, A.logical_shift_right, A.bitwise_and)
    ts(T.kk[:, 2:3], T.pi[:, :], 31, None, A.bitwise_and)
    ts(T.kk[:, 3:4], T.pi[:, :], 15, None, A.bitwise_and)
    ts(T.kk[:, 4:5], T.pi[:, :], 4, 1, A.logical_shift_right, A.bitwise_and)
    ts(T.r1[:, :], T.r1i[:, :], 7, None, A.bitwise_and)
    ts(T.r2[:, :], T.r2i[:, :], 7, None, A.bitwise_and)
    vec.wait_ge(sem.le, 128)
    ts(T.cm[:, :], T.c1b[:, :], 8, None, A.mult)
    fence()
    cp(T.bo[:, 16:32], T.bo[:, 0:16])
    cp(T.kf[:, 0:5], T.kk[:, 0:5])
    tt(T.cs[:, :], T.cm[:, :], T.c2b[:, :], A.add)
    fence()
    V(vec.transpose(T.bt[:, :], T.bo[:, :]))
    ts(ISS, TY, 1.0, None, A.is_equal)
    ts(ISF, TY, 0.0, None, A.is_equal)
    ts(ISN, TY, 2.0, None, A.is_equal)
    ts(T.tb[:, :], T.r1[:, :], 2.0, None, A.is_equal)
    fence()
    ts(fc(7), UO, -1.0, 1.0, A.mult, A.add)
    ts(T.te[:, :], T.r1[:, :], UO, None, A.is_equal)
    ts(T.eq2[:, :], T.r2[:, :], UO, None, A.is_equal)
    ts(fc(9), ISS, -1.0, 1.0, A.mult, A.add)
    fence()
    ts(fc(8), fc(7), ISS, UO, A.mult, A.add)
    cp(T.cu[:, :], T.cs[:, :])
    ts(T.eqb[:, :], T.eq2[:, :], ISS, None, A.mult)
    ts(T.eqa[:, :], T.eq2[:, :], fc(9), None, A.max)
    fence()
    ts(T.ta[:, :], T.r1[:, :], fc(8), None, A.is_equal)
    tt(T.tib[:, :], T.tb[:, :], T.eqb[:, :], A.mult)
    fence()
    tt(T.tia[:, :], T.ta[:, :], T.eqa[:, :], A.mult)
    m2 = fence()

    act.wait_ge(sem.p, px)
    S(act.activation(T.win[:, :], T.x16[:, :], Copy, scale=0.0))
    S(act.activation(T.vv[:, :], T.x16[:, 0:32], Copy, scale=0.0))
    act.wait_ge(sem.v, m2)
    for out, tab in ((T.ga, T.ta), (T.gb, T.tb), (T.gia, T.tia), (T.gib, T.tib), (T.ge, T.te)):
        S(act.activation(out[:, :], tab[:, 0:64].indirect(T.cu[:, 0:8]), Copy))
    a1 = an[0]
    act.dma_start(T.wt[:, :], T.w[:, :]).then_inc(sem.lw, 16)

    fill(T.zt[:, 0:128], 0.0)
    fill(T.land1[:, 0:8], 0.0)
    tt(fc(10), ISS, ISF, A.subtract)
    ts(fc(11), TY, -64.0, 174.0, A.mult, A.add)
    ts(fc(12), KAP8, 48.0, -1.0, A.mult, A.add)
    ts(fc(13), UO, -1.0, 8.0, A.mult, A.add)
    ts(fc(14), UO, 0.0, -8.0, A.is_equal, A.mult)
    ts(fc(15), HALF, 16.0, None, A.mult)
    fence()
    ts(T.land1[:, 0:1], ISS, 225.0, 30.0, A.mult, A.add)
    fill(T.land1[:, 1:2], 255.0)
    tt(fc(16), fc(13), fc(14), A.add)
    fence()
    ts(fc(17), TY, 8.0, fc(16), A.mult, A.add)
    ts(fc(18), fc(16), -8.0, ISN, A.add, A.mult)
    ts(fc(19), ISN, -8.0, 1.0, A.mult, A.add)
    fence()
    ts(fc(20), fc(18), 16.0, None, A.add)
    tt(fc(21), fc(17), fc(19), A.add)
    vec.wait_ge(sem.a, a1)
    scan(T.ca[:, :], T.ga[:, :], T.zt[:, 0:128], 0.0, A.add)
    scan(T.cb[:, :], T.gb[:, :], T.zt[:, 0:128], 0.0, A.add)
    V(vec.tensor_reduce(fc(22), T.ge[:, :], X, A.add))
    fence()
    ts(T.ya1[:, :], T.ca[:, :], fc(10), fc(11), A.mult, A.add)
    ts(T.yb1[:, :], T.cb[:, :], 110.0, None, A.add)
    ts(fc(23), fc(22), ISS, fc(12), A.mult, A.add)
    fence()
    tt(T.ya[:, :], T.ya1[:, :], T.gia[:, :], A.mult)
    tt(T.yb[:, :], T.yb1[:, :], T.gib[:, :], A.mult)
    BASE = fc(23)
    ts(fc(33), BASE, -1.0, None, A.mult)
    vec.wait_ge(sem.p, p2)
    ts(T.c2c[:, 0:32], T.ic[:, :], fc(17), None, A.is_gt)
    ts(T.cda[:, :], T.ic[:, :], fc(20), None, A.is_equal)
    ts(T.cdb[:, :], T.ic[:, :], fc(21), None, A.is_equal)
    ts(T.kp[:, 0:128], T.k32[:, 0:128], 1.0, None, A.min)
    ts(T.kr[:, :], T.x16[:, :], R16, 256.0, A.is_gt, A.mult)
    ts(T.sc0[:, :], T.x16[:, 0:16], R16, 1.0 / 256.0, A.is_gt, A.mult)
    ts(T.sc1[:, :], T.x16[:, 0:16], R16, None, A.is_equal)
    ts(T.val[:, :], T.val0[:, :], fc(15), None, A.add)
    fence()
    tt(T.c2c[:, 32:64], T.cda[:, :], T.cdb[:, :], A.subtract)
    scan(T.scl[:, :], T.sc0[:, :], T.sc1[:, :], 0.0, A.mult)
    vec.wait_ge(sem.lx, 16)
    V(vec.quantize_mx(T.xq[:, 0:128], T.xz[:, 0:128], T.xt[:, :]))
    fence()

    n1 = n2 = 0
    for u in range(1, N):
        here = u in order(T, topo, (s - u) % N)[1]
        n1 += 2 if here else 8
        n2 += 2 if here else 4
    vec.wait_ge(sem.i1, n1)
    V(vec.tensor_reduce(fc(24), T.land1[:, 0:22:2], X, A.add))
    V(vec.tensor_reduce(fc(25), T.land1[:, 1:22:2], X, A.add))
    fence()
    ts(T.xa[:, :], T.ya[:, :], fc(24), None, A.is_ge)
    ts(T.xb[:, :], T.yb[:, :], fc(25), None, A.is_ge)
    fence()
    scan(T.cum[:, :], T.xa[:, :], T.xb[:, :], BASE, A.add)
    tt(T.xs[:, :], T.xa[:, :], T.xb[:, :], A.add)
    mc = fence()
    act.wait_ge(sem.v, mc)
    S(act.activation(fc(26), T.cum[:, 127:128], Ident, bias=fc(33)))
    act.wait_ge(sem.a, an[0])
    S(act.activation(T.e2[:, :], T.c2c[:, :], Copy, scale=fc(26)))
    tt(T.mm[:, :], T.xs[:, :], T.cum[:, :], A.mult)
    fence()
    V(vec.transpose(T.mt[:, :], T.mm[:, :]))
    fence()
    scan(T.ss[:, :], T.kp[:, 0:128], T.mt[:, :], 0.0, A.mult)
    vec.wait_ge(sem.a, an[0])
    V(vec.transpose(T.e2t[:, :], T.e2[:, :]))
    fence()
    cp(T.so[:, :], T.ss[:, 15:128:32])
    tt(T.info2[:, 0:16:2], T.e2t[:, 0:8], T.e2t[:, 8:16], A.add)
    tt(T.e2s[:, :], T.e2t[:, 32:40], T.e2t[:, 40:48], A.add)
    m3 = fence()
    vec.tensor_tensor(T.info2[:, 1:16:2], T.e2s[:, :], T.e2t[:, 48:56], A.add).then_inc(sem.n2, 1)
    cp(T.win[:, 0:384].indirect(T.so[:, 0:4]), T.val[:, :])
    fence()
    scan(T.rr[:, :], T.kr[:, :], T.win[:, :], 0.0, A.mult)
    fence()
    ts(T.vv[:, 0:16:2], T.rr[:, 15:384:48], T.scl[:, 15:16], None, A.mult)
    ts(T.vv[:, 1:16:2], T.rr[:, 31:384:48], T.scl[:, 15:16], None, A.mult)
    fence()
    V(vec.transpose(T.vt[:, :], T.vv[:, :]))
    fence()
    tt(T.v2[:, 0:16], T.vt[:, 0:16], T.vt[:, 16:32], A.add)
    tt(T.v2[:, 16:32], T.vt[:, 0:16], T.vt[:, 16:32], A.add)
    fence()
    V(vec.transpose(T.vb[:, :], T.v2[:, :]))
    fence()
    cp(T.offp[:, :], T.vb[:, 0:16])
    m4 = fence()

    xc = lambda a, b: T.xq[:, 0:128].bitcast(dt.uint32).indirect(T.offp[:, a:b])
    xz = lambda a, b: T.xz[:, 0:128].indirect(T.offp[:, a:b])
    vec.tensor_copy(T.oq[:, 32:160].bitcast(dt.uint32), xc(2, 10)).then_inc(sem.pc1, 1)
    vec.tensor_copy(T.oq[:, 160:256].bitcast(dt.uint32), xc(10, 16)).then_inc(sem.pc2, 1)
    cp(T.lq[:, 0:32].bitcast(dt.uint32), xc(0, 2))
    act.wait_ge(sem.v, m4)
    act.activation(T.oz[:, 32:160], xz(2, 10), Copy).then_inc(sem.pa1, 1)
    act.activation(T.oz[:, 160:256], xz(10, 16), Copy).then_inc(sem.pa2, 1)
    S(act.activation(T.lz[:, 0:32], xz(0, 2), Copy))

    g.wait_ge(sem.v, m3)
    g.wait_ge(sem.n2, 1)
    g.remote_dma_fused([xfer(core, rc[h], topo, half[h], sem.i2, T.info2[:, 2 + 4 * h:6 + 4 * h], T.hand2[:, :])
                        for h in range(2)], local_sem=sem.lo)
    to_plane(T.info2, T.land2, sem.i2)
    g.wait_ge(sem.pc1, 1)
    g.remote_dma_fused([xfer(core, rc[h], topo, (off, on)[h], sem.tc, T.oq[:, 32 + 64 * h:96 + 64 * h].bitcast(dt.uint8),
                             T.rq[:, :].bitcast(dt.uint8)) for h in range(2)], local_sem=sem.lo)
    g.wait_ge(sem.pa1, 1)
    g.remote_dma_fused([xfer(core, rs[h], topo, half[h], sem.ts, T.oz[:, 32 + 64 * h:96 + 64 * h],
                             T.rz[:, :]) for h in range(2)], local_sem=sem.lo)
    g.wait_ge(sem.pc2, 1)
    tr = []
    for i, u in enumerate(direct):
        b, c = W * ords.index(u), W * slot_of(u)
        x, y = SPLIT_C[i]
        tr.append(xfer(core, at(T, topo, s, u), topo, off[x:y], sem.tc, T.oq[:, b:b + W].bitcast(dt.uint8),
                       T.lq[:, c:c + W].bitcast(dt.uint8)))
    g.remote_dma_fused(tr, local_sem=sem.lo)
    g.wait_ge(sem.pa2, 1)
    tr = []
    for i, u in enumerate(direct):
        b, c = W * ords.index(u), W * slot_of(u)
        x, y = SPLIT_S[i]
        tr.append(xfer(core, at(T, topo, s, u), topo, off[x:y], sem.ts, T.oz[:, b:b + W], T.lz[:, c:c + W]))
    g.remote_dma_fused(tr, local_sem=sem.lo)
    g.wait_ge(sem.lo, 22 + 14 + 16 + 3 * 8)

    fill(T.zt[:, 128:640], 0.0)
    fill(T.land2[:, 0:8], 0.0)
    ts(T.kp[:, 128:320], T.k32[:, 128:320], 1.0, None, A.min)
    fence()
    V(vec.quantize_mx(T.lq[:, LAND:LAND + ROOM], T.lz[:, LAND:LAND + ROOM], T.zt[:, :]))
    vec.wait_ge(sem.n2, 1)
    cp(T.land2[:, 0:2], T.info2[:, 0:2])
    ts(fc(27), K32, 1.0, 32.0, A.is_ge, A.mult)
    ts(fc(28), K32, 17.0, -32.0, A.is_ge, A.mult)
    ts(fc(29), K32, 8.0, -256.0, A.is_equal, A.mult)
    ts(T.jw[:, :], T.jw0[:, :], R16, None, A.add)
    fence()
    tt(fc(30), fc(27), fc(28), A.add)
    fence()
    tt(T.land2[:, 3:4], fc(30), fc(29), A.add)
    vec.wait_ge(sem.lw, 16)
    for o in range(O):
        V(vec.quantize_mx(T.wq[:, 128 * o:128 * o + 128], T.wz[:, 128 * o:128 * o + 128], T.wt[:, 512 * o:512 * o + 512]))
    fence()

    vec.wait_ge(sem.p, p3)
    vec.wait_ge(sem.i2, n2)
    V(vec.tensor_reduce(fc(31), T.land2[:, 0:22:2], X, A.add))
    V(vec.tensor_reduce(fc(32), T.land2[:, 1:22:2], X, A.add))
    fence()
    ts(T.st[:, :], T.jd[:, :], fc(31), fc(32), A.is_ge, A.mult)
    fence()
    V(vec.transpose(T.stt[:, :], T.st[:, :]))
    fence()
    scan(T.sw[:, :], T.kp[:, :], T.stt[:, :], 0.0, A.mult)
    fence()
    tt(T.wl[:, :], T.sw[:, 31:320:32], T.jw[:, :], A.add)
    fence()
    cp(T.offh[:, :], T.wl[:, :])
    m5 = fence()

    nt = 0
    for u in range(1, N):
        d = order(T, topo, (s - u) % N)[1]
        nt += SPLIT_C[d.index(u)][1] - SPLIT_C[d.index(u)][0] if u in d else 4
    act.wait_ge(sem.v, m5)
    act.wait_ge(sem.a, an[0])
    act.wait_ge(sem.ts, nt)
    S(act.activation(T.hz[:, 0:160], T.lz[:, 0:416].indirect(T.offh[:, 0:10]), Copy))
    a2 = an[0]
    vec.wait_ge(sem.tc, nt)
    cp(T.hq[:, 0:160].bitcast(dt.uint32), T.lq[:, 0:416].bitcast(dt.uint32).indirect(T.offh[:, 0:10]))
    m6 = vn[0]
    ten.wait_ge(sem.v, m6)
    ten.wait_ge(sem.a, a2)
    for o in range(O):
        ten.matmul_mx(T.ps[:, 512 * o:512 * o + ROOM], T.wq[:, 128 * o:128 * o + 128], T.wz[:, 128 * o:128 * o + 128],
                      T.hq[:, 0:ROOM], T.hz[:, 0:ROOM], True, True).then_inc(sem["t%d" % o], 1)
    for o in range(O):
        y, p = T.ys[:, ROOM * o:ROOM * o + ROOM], T.ps[:, 512 * o:512 * o + ROOM]
        if o % 2 == 0:
            vec.wait_ge(sem["t%d" % o], 1)
            vec.tensor_copy(y, p).then_inc(sem["y%d" % o], 1)
        else:
            act.wait_ge(sem["t%d" % o], 1)
            act.activation(y, p, Copy).then_inc(sem["y%d" % o], 1)
    for q, o, e in ((g.sync, 0, 1), (act, 1, 4)):
        for k in range(o, e):
            q.wait_ge(sem["y%d" % k], 1)
        q.dma_start(T.y[:, ROOM * o:ROOM * e], T.ys[:, ROOM * o:ROOM * e]).then_inc(sem.ly, 16)
    act.wait_ge(sem.ly, 32)
